import numpy as np
import ml_dtypes


def mxq(x, axis, fmt="e4m3"):
    dtype, down = {"e4m3": (ml_dtypes.float8_e4m3fn, 7), "e5m2": (ml_dtypes.float8_e5m2, 14)}[fmt]
    v = np.moveaxis(np.asarray(x, np.float32).astype(ml_dtypes.bfloat16).astype(np.float64), axis, -1)
    blocks = v.reshape(v.shape[:-1] + (-1, 32))
    amax = np.abs(blocks).max(-1, keepdims=True)
    byte = np.maximum(np.where(amax > 0, np.frexp(amax)[1] - 1 + 127, 0) - down, 1)
    scale = np.exp2(byte - 127.0)
    codes = (blocks / scale).astype(np.float32).astype(dtype).astype(np.float64)
    return np.moveaxis((codes * scale).reshape(v.shape), -1, axis)


WIDE = False


def mx_kscale(k):
    if not WIDE:
        return np.ones(k)
    levels = np.array([10, -10, 5, -5, 0])
    if k % 512:
        return np.exp2(np.random.permutation(np.resize(levels, k // 32))).repeat(32)
    a = np.empty((k // 512, 16))
    for p in range(k // 512):
        a[p, :8] = np.random.permutation(np.resize(levels, 8))
        for g in range(8):
            far = levels[np.abs(levels - a[p, g]) >= 10]
            a[p, g + 8] = far[np.random.randint(len(far))]
    return np.exp2(a.ravel()).repeat(32)


def f64(x):
    return np.asarray(x).astype(np.float64)


E2M1 = np.array([0.0, 0.5, 1.0, 1.5, 2.0, 3.0, 4.0, 6.0, -0.0, -0.5, -1.0, -1.5, -2.0, -3.0, -4.0, -6.0])


def pack_weight(w, fmt):
    k, n = w.shape
    w = f64(np.asarray(w, np.float32).astype(ml_dtypes.bfloat16)).reshape(k // 32, 32, n)
    amax = np.abs(w).max(1)
    if fmt == "e4m3":
        byte = np.frexp(amax)[1] - 1 + 127 - 7
    else:
        mant, ex = np.frexp(amax / 6.0)
        byte = np.where(mant > 0.5, ex, ex - 1) + 127
    byte = np.clip(np.where(amax > 0, byte, 1), 1, 254)
    scaled = (w * np.exp2(127.0 - byte)[:, None, :]).reshape(k, n).astype(np.float32)
    by_word = np.ascontiguousarray(scaled.reshape(k // 512, 128, 4, n).transpose(0, 1, 3, 2))
    if fmt == "e4m3":
        words = by_word.astype(ml_dtypes.float8_e4m3fn).view(np.uint8)
    else:
        c = by_word.astype(ml_dtypes.float4_e2m1fn).view(np.uint8) & 0xF
        words = (c[..., 0::2] | (c[..., 1::2] << 4)).reshape(k // 512, 128, 2 * n)
    return np.ascontiguousarray(words), np.ascontiguousarray(byte.astype(np.uint8).reshape(k // 512, 16, n))


def unpack_weight(words, scales, fmt):
    g, _, n = scales.shape
    words = np.ascontiguousarray(words).reshape(g, 128, n, -1)
    if fmt == "e4m3":
        vals = words.view(ml_dtypes.float8_e4m3fn).astype(np.float64)
    else:
        nib = np.empty((g, 128, n, 4), np.uint8)
        nib[..., 0::2] = words & 0xF
        nib[..., 1::2] = words >> 4
        vals = E2M1[nib]
    vals = vals * np.repeat(np.exp2(scales.astype(np.float64) - 127.0), 8, axis=1)[..., None]
    return vals.transpose(0, 1, 3, 2).reshape(g * 512, n)


K, L, T, R, N = 1024, 512, 512, 512, 512


def setup_inputs():
    n = np.random.standard_normal
    fk = mx_kscale(K)
    fl = mx_kscale(L)
    fr = mx_kscale(R)
    xtp = pack_weight(n((K, T)) * np.random.uniform(0.3, 1.9, (1, T)) / fk[:, None], "e4m3")
    wap = pack_weight(n((K, R)) * 1 / np.sqrt(K) * fk[:, None], "e2m1")
    xqp = pack_weight(n((L, T)) * 0.5 / fl[:, None], "e2m1")
    wcp = pack_weight(n((L, R)) * 1 / np.sqrt(L) * fl[:, None], "e4m3")
    wbp = pack_weight(n((R, N)) * 1 / np.sqrt(R) / fr[:, None], "e2m1")
    wyp = pack_weight(n((K, N)) * 1 / np.sqrt(K) * fk[:, None], "e4m3")
    return {
        "xt_words": xtp[0],
        "xt_scales": xtp[1],
        "wa_words": wap[0],
        "wa_scales": wap[1],
        "xq_words": xqp[0],
        "xq_scales": xqp[1],
        "wc_words": wcp[0],
        "wc_scales": wcp[1],
        "fr": (np.random.uniform(0.5, 2.0, (R, 1)) * fr[:, None]).astype(np.float32),
        "wb_words": wbp[0],
        "wb_scales": wbp[1],
        "wy_words": wyp[0],
        "wy_scales": wyp[1],
    }


def reference(xt_words, xt_scales, wa_words, wa_scales, xq_words, xq_scales, wc_words, wc_scales, fr, wb_words, wb_scales, wy_words, wy_scales):
    xtu = unpack_weight(xt_words, xt_scales, "e4m3")
    wau = unpack_weight(wa_words, wa_scales, "e2m1")
    xqu = unpack_weight(xq_words, xq_scales, "e2m1")
    wcu = unpack_weight(wc_words, wc_scales, "e4m3")
    wbu = unpack_weight(wb_words, wb_scales, "e2m1")
    wyu = unpack_weight(wy_words, wy_scales, "e4m3")
    z = xtu.T @ wau + xqu.T @ wcu
    e = np.mean(np.square(z), axis=1, keepdims=True)
    h1 = z * e / (e + 1.0)
    ht = h1.T
    hid = ht * f64(fr)
    hidq = mxq(hid, 0, "e4m3")
    y = wbu.T @ hidq + wyu.T @ xtu
    return y

@@ -1,0 +1,243 @@
+from contextlib import ExitStack
+
+import concourse.mybir as mybir
+from concourse.masks import make_identity
+
+K, L, T, R, N = 1024, 512, 512, 512, 512
+FLOPS = 2 * T * (K * R + L * R + R * N + K * N)
+
+F32 = mybir.dt.float32
+BF16 = mybir.dt.bfloat16
+I32 = mybir.dt.int32
+U32 = mybir.dt.uint32
+U8 = mybir.dt.uint8
+FP8X4 = mybir.dt.float8_e4m3fn_x4
+FP4X4 = mybir.dt.float4_e2m1fn_x4
+ALU = mybir.AluOpType
+ACT = mybir.ActivationFunctionType
+
+P = 128
+W = 512
+TILES = T // P
+
+
+def tile_mix_hidden_by_row_energy_kernel(
+    tc, xt_words, xt_scales, wa_words, wa_scales, xq_words, xq_scales, wc_words, wc_scales,
+    fr, wb_words, wb_scales, wy_words, wy_scales, out,
+):
+    nc = tc.nc
+
+    with ExitStack() as ctx:
+        sb = ctx.enter_context(tc.tile_pool(name="sb", bufs=1))
+        ps = ctx.enter_context(tc.psum_pool(name="ps", bufs=1))
+        ctx.enter_context(tc.manual_schedule())
+
+        def load_rows(queue, rows, first, scales):
+            passes = scales.shape[0]
+            dst = rows[:, first * W : (first + passes) * W].bitcast(I32)
+            queue.dma_start(
+                out=dst.rearrange("q (z n) -> q z n", z=passes),
+                in_=scales.bitcast(I32).rearrange("z q n -> q z n"),
+            )
+
+        def spread_rows(queue, planes, rows):
+            for q in range(4):
+                queue.dma_start(
+                    out=planes[32 * q : 32 * q + 4, :].bitcast(I32),
+                    in_=rows[4 * q : 4 * q + 4, :].bitcast(I32),
+                )
+
+        def load_fp8(name, words):
+            passes = words.shape[0]
+            codes = sb.tile([P, passes * W], U32, name=name, align_bytes=64)
+            nc.sync.dma_start(
+                out=codes[:].bitcast(I32).rearrange("p (z n) -> p z n", z=passes),
+                in_=words.rearrange("z p n j -> p z (n j)").bitcast(I32),
+            )
+            return codes
+
+        def load_fp4(name, words):
+            passes = words.shape[0]
+            codes = sb.tile([P, passes * 2 * W], U8, name=name, align_bytes=64)
+            nc.sync.dma_start(
+                out=codes[:].bitcast(I32).rearrange("p (z n) -> p z n", z=passes),
+                in_=words.rearrange("z p b -> p z b").bitcast(I32),
+            )
+            return codes
+
+        def fp8(codes, z, first, count):
+            return codes[:, z * W + first : z * W + first + count].bitcast(FP8X4)
+
+        def fp4(codes, z, first, count):
+            return codes[:, 2 * (z * W + first) : 2 * (z * W + first + count)].bitcast(FP4X4)
+
+        def plane(planes, index, first, count):
+            return planes[:, index * W + first : index * W + first + count]
+
+        XQ, WC, XT, WA = 0, 1, 2, 4
+        WY, WB = 0, 2
+        rows_a = sb.tile([16, 6 * W], U8, name="rows_a")
+        rows_b = sb.tile([16, 3 * W], U8, name="rows_b")
+        planes_a = sb.tile([P, 6 * W], U8, name="planes_a", align_bytes=64)
+        planes_b = sb.tile([P, 3 * W], U8, name="planes_b", align_bytes=64)
+        nc.vector.memset(planes_a[:].bitcast(I32), 0)
+        nc.vector.memset(planes_b[:].bitcast(I32), 0)
+        one = sb.tile([P, 1], F32, name="one")
+        nc.vector.memset(one[:], 1.0)
+
+        load_rows(nc.scalar, rows_a, XQ, xq_scales)
+        load_rows(nc.scalar, rows_a, WC, wc_scales)
+        load_rows(nc.scalar, rows_a, XT, xt_scales)
+        load_rows(nc.scalar, rows_a, WA, wa_scales)
+        xq = load_fp4("xq", xq_words)
+        wc = load_fp8("wc", wc_words)
+        xt = load_fp8("xt", xt_words)
+        wa = load_fp4("wa", wa_words)
+        spread_rows(nc.scalar, planes_a, rows_a)
+
+        fr_cols = sb.tile([P, 4], F32, name="fr_cols")
+        nc.gpsimd.dma_start(out=fr_cols[:], in_=fr.rearrange("(p j) o -> p (j o)", j=4))
+        ident = sb.tile([P, P], F32, name="ident")
+        make_identity(nc, ident[:])
+        load_rows(nc.gpsimd, rows_b, WY, wy_scales)
+        load_rows(nc.gpsimd, rows_b, WB, wb_scales)
+
+        wy = load_fp8("wy", wy_words)
+        wb = load_fp4("wb", wb_words)
+        spread_rows(nc.sync, planes_b, rows_b)
+
+        warm = sb.tile([P, 1], F32, name="warm")
+        nc.scalar.activation(out=warm[:], in_=one[:], func=ACT.Square)
+
+        fr_ps = ps.tile([P, 4, P], F32, name="fr_ps", tag="bank7")
+        for j in range(4):
+            nc.tensor.transpose(fr_ps[:, j, :], fr_cols[:, j : j + 1].to_broadcast([P, P]), ident[:])
+        fr_rows = sb.tile([P, 2, P, 2], F32, name="fr_rows")
+        nc.vector.tensor_copy(out=fr_rows[:], in_=fr_ps[:].rearrange("m (u e) p -> m u p e", e=2))
+
+        z = [ps.tile([P, R], F32, name="z%d" % i, tag="bank%d" % i) for i in range(TILES)]
+        for i in range(TILES):
+            nc.tensor.matmul_mx(
+                out=z[i][:], lhsT=fp4(xq, 0, i * P, P), lhsT_scale=plane(planes_a, XQ, i * P, P),
+                rhs=fp8(wc, 0, 0, R), rhs_scale=plane(planes_a, WC, 0, R), start=True, stop=False,
+            )
+        for i in range(TILES):
+            for c in range(2):
+                nc.tensor.matmul_mx(
+                    out=z[i][:], lhsT=fp8(xt, c, i * P, P), lhsT_scale=plane(planes_a, XT + c, i * P, P),
+                    rhs=fp4(wa, c, 0, R), rhs_scale=plane(planes_a, WA + c, 0, R), start=False, stop=(c == 1),
+                )
+
+        squares = sb.tile([P, R], BF16, name="squares")
+        total = [sb.tile([P, 1], F32, name="total%d" % i) for i in range(TILES)]
+        for i in range(TILES):
+            nc.scalar.activation(out=squares[:], in_=z[i][:], func=ACT.Square, accum_out=total[i][:])
+
+        denom = [sb.tile([P, 1], F32, name="denom%d" % i) for i in range(TILES)]
+        recip = [sb.tile([P, 1], F32, name="recip%d" % i) for i in range(TILES)]
+        gain = [sb.tile([P, 1], F32, name="gain%d" % i) for i in range(TILES)]
+        hid = [[sb.tile([P, R // 2], BF16, name="hid%d_%d" % (i, u)) for u in range(2)] for i in range(TILES)]
+        grouped = [sb.tile([P, R], BF16, name="grouped%d" % i, align_bytes=64) for i in range(TILES)]
+        codes = [sb.tile([P, P], U32, name="codes%d" % i, align_bytes=64) for i in range(TILES)]
+        scales = [sb.tile([P, P], U8, name="scales%d" % i, align_bytes=64) for i in range(TILES)]
+        result = [sb.tile([P, 4, P], F32, name="result%d" % i) for i in range(TILES)]
+        turned = {}
+        y = {}
+        out_tiles = out.rearrange("(a p) t -> p a t", p=P)
+
+        def step_denom(i):
+            nc.vector.tensor_scalar(out=denom[i][:], in0=total[i][:], scalar1=float(R), scalar2=None, op0=ALU.add)
+
+        def step_recip(i):
+            nc.vector.reciprocal(out=recip[i][:], in_=denom[i][:])
+
+        def step_gain(i):
+            nc.vector.tensor_tensor(out=gain[i][:], in0=total[i][:], in1=recip[i][:], op=ALU.mult)
+
+        def weigh(i, u):
+            nc.vector.scalar_tensor_tensor(
+                out=hid[i][u][:].rearrange("t (p e) -> t p e", e=2),
+                in0=z[i][:].rearrange("t (p u e) -> t u p e", u=2, e=2)[:, u],
+                scalar=gain[i][:], in1=fr_rows[:, u], op0=ALU.mult, op1=ALU.mult,
+            )
+
+        def turn(i):
+            turned[i] = ps.tile([P, 2, P], F32, name="turned%d" % i, tag="bank%d" % i)
+            for u in range(2):
+                nc.tensor.transpose(turned[i][:, u, :], hid[i][u][:].bitcast(F32), ident[:])
+
+        def interleave(i):
+            nc.scalar.copy(
+                out=grouped[i][:].bitcast(F32).rearrange("p (t u) -> p t u", u=2),
+                in_=turned[i][:].rearrange("p u t -> p t u"),
+            )
+
+        def quantise(i):
+            nc.vector.quantize_mx(out=codes[i][:].bitcast(FP8X4), scales=scales[i][:], in_=grouped[i][:])
+
+        def skip(i):
+            y[i] = ps.tile([P, 4, P], F32, name="y%d" % i, tag="bank%d" % (4 + i))
+            for a in range(4):
+                for c in range(2):
+                    nc.tensor.matmul_mx(
+                        out=y[i][:, a, :], lhsT=fp8(wy, c, a * P, P), lhsT_scale=plane(planes_b, WY + c, a * P, P),
+                        rhs=fp8(xt, c, i * P, P), rhs_scale=plane(planes_a, XT + c, i * P, P),
+                        start=(a == 0 and c == 0), stop=False,
+                    )
+
+        def second(i):
+            for a in range(4):
+                nc.tensor.matmul_mx(
+                    out=y[i][:, a, :], lhsT=fp4(wb, 0, a * P, P), lhsT_scale=plane(planes_b, WB, a * P, P),
+                    rhs=codes[i][:].bitcast(FP8X4), rhs_scale=scales[i][:], start=False, stop=(a == 3),
+                )
+
+        def store(i, on_scalar):
+            if on_scalar:
+                nc.scalar.copy(out=result[i][:], in_=y[i][:])
+            else:
+                nc.vector.tensor_copy(out=result[i][:], in_=y[i][:])
+            nc.sync.dma_start(out=out_tiles[:, :, i * P : (i + 1) * P], in_=result[i][:])
+
+        def weigh_tile(i):
+            more = i + 1 < TILES
+            if more:
+                step_denom(i + 1)
+            weigh(i, 0)
+            if more:
+                step_recip(i + 1)
+            weigh(i, 1)
+            if more:
+                step_gain(i + 1)
+
+        step_denom(0)
+        step_recip(0)
+        step_gain(0)
+        skip(0)
+        weigh_tile(0)
+        turn(0)
+        interleave(0)
+        skip(1)
+        weigh_tile(1)
+        turn(1)
+        interleave(1)
+        quantise(0)
+        second(0)
+        skip(2)
+        weigh_tile(2)
+        store(0, True)
+        weigh_tile(3)
+        quantise(1)
+        turn(2)
+        turn(3)
+        interleave(2)
+        interleave(3)
+        second(1)
+        skip(3)
+        quantise(2)
+        store(1, True)
+        quantise(3)
+        second(2)
+        second(3)
+        store(2, False)
+        store(3, True)

@@ -40,9 +40,9 @@ def tile_mix_hidden_by_row_energy_kernel(
                 in_=scales.bitcast(I32).rearrange("z q n -> q z n"),
             )
 
-        def spread_rows(queue, planes, rows):
+        def spread_rows(queues, planes, rows):
             for q in range(4):
-                queue.dma_start(
+                queues[q % 2].dma_start(
                     out=planes[32 * q : 32 * q + 4, :].bitcast(I32),
                     in_=rows[4 * q : 4 * q + 4, :].bitcast(I32),
                 )
@@ -85,26 +85,25 @@ def tile_mix_hidden_by_row_energy_kernel(
         one = sb.tile([P, 1], F32, name="one")
         nc.vector.memset(one[:], 1.0)
 
-        load_rows(nc.scalar, rows_a, XQ, xq_scales)
-        load_rows(nc.scalar, rows_a, WC, wc_scales)
+        load_rows(nc.sync, rows_a, XQ, xq_scales)
         load_rows(nc.scalar, rows_a, XT, xt_scales)
+        load_rows(nc.sync, rows_a, WC, wc_scales)
         load_rows(nc.scalar, rows_a, WA, wa_scales)
+        fr_cols = sb.tile([P, 4], F32, name="fr_cols")
+        nc.sync.dma_start(out=fr_cols[:], in_=fr.rearrange("(p j) o -> p (j o)", j=4))
         xq = load_fp4("xq", xq_words)
         wc = load_fp8("wc", wc_words)
-        xt = load_fp8("xt", xt_words)
         wa = load_fp4("wa", wa_words)
-        spread_rows(nc.scalar, planes_a, rows_a)
-
-        fr_cols = sb.tile([P, 4], F32, name="fr_cols")
-        nc.gpsimd.dma_start(out=fr_cols[:], in_=fr.rearrange("(p j) o -> p (j o)", j=4))
-        ident = sb.tile([P, P], F32, name="ident")
-        make_identity(nc, ident[:])
-        load_rows(nc.gpsimd, rows_b, WY, wy_scales)
-        load_rows(nc.gpsimd, rows_b, WB, wb_scales)
-
+        spread_rows([nc.sync, nc.scalar], planes_a, rows_a)
+        xt = [load_fp8("xt%d" % c, xt_words[c : c + 1]) for c in range(2)]
+        load_rows(nc.sync, rows_b, WY, wy_scales)
+        load_rows(nc.sync, rows_b, WB, wb_scales)
         wy = load_fp8("wy", wy_words)
         wb = load_fp4("wb", wb_words)
-        spread_rows(nc.sync, planes_b, rows_b)
+        spread_rows([nc.sync, nc.sync], planes_b, rows_b)
+
+        ident = sb.tile([P, P], F32, name="ident")
+        make_identity(nc, ident[:])
 
         warm = sb.tile([P, 1], F32, name="warm")
         nc.scalar.activation(out=warm[:], in_=one[:], func=ACT.Square)
@@ -124,7 +123,7 @@ def tile_mix_hidden_by_row_energy_kernel(
         for i in range(TILES):
             for c in range(2):
                 nc.tensor.matmul_mx(
-                    out=z[i][:], lhsT=fp8(xt, c, i * P, P), lhsT_scale=plane(planes_a, XT + c, i * P, P),
+                    out=z[i][:], lhsT=fp8(xt[c], 0, i * P, P), lhsT_scale=plane(planes_a, XT + c, i * P, P),
                     rhs=fp4(wa, c, 0, R), rhs_scale=plane(planes_a, WA + c, 0, R), start=False, stop=(c == 1),
                 )
 
@@ -140,7 +139,7 @@ def tile_mix_hidden_by_row_energy_kernel(
         grouped = [sb.tile([P, R], BF16, name="grouped%d" % i, align_bytes=64) for i in range(TILES)]
         codes = [sb.tile([P, P], U32, name="codes%d" % i, align_bytes=64) for i in range(TILES)]
         scales = [sb.tile([P, P], U8, name="scales%d" % i, align_bytes=64) for i in range(TILES)]
-        result = [sb.tile([P, 4, P], F32, name="result%d" % i) for i in range(TILES)]
+        Y_BANKS = [[4], [5], [6], [7, 0]]
         turned = {}
         y = {}
         out_tiles = out.rearrange("(a p) t -> p a t", p=P)
@@ -176,28 +175,33 @@ def tile_mix_hidden_by_row_energy_kernel(
             nc.vector.quantize_mx(out=codes[i][:].bitcast(FP8X4), scales=scales[i][:], in_=grouped[i][:])
 
         def skip(i):
-            y[i] = ps.tile([P, 4, P], F32, name="y%d" % i, tag="bank%d" % (4 + i))
+            banks = Y_BANKS[i]
+            per = 4 // len(banks)
+            y[i] = [ps.tile([P, per, P], F32, name="y%d_%d" % (i, b), tag="bank%d" % b) for b in banks]
             for a in range(4):
                 for c in range(2):
                     nc.tensor.matmul_mx(
-                        out=y[i][:, a, :], lhsT=fp8(wy, c, a * P, P), lhsT_scale=plane(planes_b, WY + c, a * P, P),
-                        rhs=fp8(xt, c, i * P, P), rhs_scale=plane(planes_a, XT + c, i * P, P),
-                        start=(a == 0 and c == 0), stop=False,
+                        out=y[i][a // per][:, a % per, :], lhsT=fp8(wy, c, a * P, P), lhsT_scale=plane(planes_b, WY + c, a * P, P),
+                        rhs=fp8(xt[c], 0, i * P, P), rhs_scale=plane(planes_a, XT + c, i * P, P),
+                        start=(a % per == 0 and c == 0), stop=False,
                     )
 
         def second(i):
+            per = 4 // len(y[i])
             for a in range(4):
                 nc.tensor.matmul_mx(
-                    out=y[i][:, a, :], lhsT=fp4(wb, 0, a * P, P), lhsT_scale=plane(planes_b, WB, a * P, P),
-                    rhs=codes[i][:].bitcast(FP8X4), rhs_scale=scales[i][:], start=False, stop=(a == 3),
+                    out=y[i][a // per][:, a % per, :], lhsT=fp4(wb, 0, a * P, P), lhsT_scale=plane(planes_b, WB, a * P, P),
+                    rhs=codes[i][:].bitcast(FP8X4), rhs_scale=scales[i][:], start=False, stop=(a % per == per - 1),
                 )
 
-        def store(i, on_scalar):
+        def store(i, part, on_scalar, queue):
+            per = 4 // len(y[i])
+            result = sb.tile([P, per, P], F32, name="result%d_%d" % (i, part))
             if on_scalar:
-                nc.scalar.copy(out=result[i][:], in_=y[i][:])
+                nc.scalar.copy(out=result[:], in_=y[i][part][:])
             else:
-                nc.vector.tensor_copy(out=result[i][:], in_=y[i][:])
-            nc.sync.dma_start(out=out_tiles[:, :, i * P : (i + 1) * P], in_=result[i][:])
+                nc.vector.tensor_copy(out=result[:], in_=y[i][part][:])
+            queue.dma_start(out=out_tiles[:, part * per : (part + 1) * per, i * P : (i + 1) * P], in_=result[:])
 
         def weigh_tile(i):
             more = i + 1 < TILES
@@ -223,9 +227,8 @@ def tile_mix_hidden_by_row_energy_kernel(
         interleave(1)
         quantise(0)
         second(0)
-        skip(2)
         weigh_tile(2)
-        store(0, True)
+        store(0, 0, True, nc.sync)
         weigh_tile(3)
         quantise(1)
         turn(2)
@@ -233,11 +236,13 @@ def tile_mix_hidden_by_row_energy_kernel(
         interleave(2)
         interleave(3)
         second(1)
-        skip(3)
+        skip(2)
         quantise(2)
-        store(1, True)
+        store(1, 0, True, nc.sync)
         quantise(3)
         second(2)
+        store(2, 0, False, nc.sync)
+        skip(3)
         second(3)
-        store(2, False)
-        store(3, True)
+        store(3, 0, True, nc.scalar)
+        store(3, 1, False, nc.sync)

@@ -19,6 +19,8 @@ ACT = mybir.ActivationFunctionType
 P = 128
 W = 512
 TILES = T // P
+HALF = T // 2
+WARM_EARLY, WARM_LATE = 8, 13
 
 
 def tile_mix_hidden_by_row_energy_kernel(
@@ -34,7 +36,7 @@ def tile_mix_hidden_by_row_energy_kernel(
 
         def load_rows(queue, rows, first, scales):
             passes = scales.shape[0]
-            dst = rows[:, first * W : (first + passes) * W].bitcast(I32)
+            dst = rows[16:32, first * W : (first + passes) * W].bitcast(I32)
             queue.dma_start(
                 out=dst.rearrange("q (z n) -> q z n", z=passes),
                 in_=scales.bitcast(I32).rearrange("z q n -> q z n"),
@@ -43,8 +45,8 @@ def tile_mix_hidden_by_row_energy_kernel(
         def spread_rows(queues, planes, rows):
             for q in range(4):
                 queues[q % 2].dma_start(
-                    out=planes[32 * q : 32 * q + 4, :].bitcast(I32),
-                    in_=rows[4 * q : 4 * q + 4, :].bitcast(I32),
+                    out=planes[q:P:32, :].bitcast(I32),
+                    in_=rows[16 + q : 32 : 4, :].bitcast(I32),
                 )
 
         def load_fp8(name, words):
@@ -76,34 +78,63 @@ def tile_mix_hidden_by_row_energy_kernel(
 
         XQ, WC, XT, WA = 0, 1, 2, 4
         WY, WB = 0, 2
-        rows_a = sb.tile([16, 6 * W], U8, name="rows_a")
-        rows_b = sb.tile([16, 3 * W], U8, name="rows_b")
+        rows_a = sb.tile([32, 6 * W], U8, name="rows_a")
+        rows_b = sb.tile([32, 3 * W], U8, name="rows_b")
         planes_a = sb.tile([P, 6 * W], U8, name="planes_a", align_bytes=64)
         planes_b = sb.tile([P, 3 * W], U8, name="planes_b", align_bytes=64)
+        idle = sb.tile([P, 4 * P], BF16, name="idle", align_bytes=64)
+        idle_codes = sb.tile([P, P], U32, name="idle_codes", align_bytes=64)
+        idle_scales = sb.tile([P, P], U8, name="idle_scales", align_bytes=64)
+        idle_ps = ps.tile([P, P], F32, name="idle_ps", tag="bank6")
+        ident = sb.tile([P, P], F32, name="ident")
+        nc.vector.memset(idle[:], 1.0)
+        nc.vector.memset(ident[:], 0.0)
+        nc.vector.quantize_mx(out=idle_codes[:].bitcast(FP8X4), scales=idle_scales[:], in_=idle[:])
+
+        def keep_busy(count):
+            for n in range(count):
+                nc.tensor.matmul_mx(
+                    out=idle_ps[:], lhsT=idle_codes[:].bitcast(FP8X4), lhsT_scale=idle_scales[:],
+                    rhs=idle_codes[:].bitcast(FP8X4), rhs_scale=idle_scales[:], start=True, stop=True,
+                )
+
+        keep_busy(WARM_EARLY)
         nc.vector.memset(planes_a[:].bitcast(I32), 0)
         nc.vector.memset(planes_b[:].bitcast(I32), 0)
         one = sb.tile([P, 1], F32, name="one")
         nc.vector.memset(one[:], 1.0)
+
+        def load_xt(half):
+            codes = sb.tile([P, 2 * HALF], U32, name="xt%d" % half, align_bytes=64)
+            words = xt_words[:, :, half * HALF : (half + 1) * HALF, :]
+            nc.sync.dma_start(
+                out=codes[:].bitcast(I32).rearrange("p (z n) -> p z n", z=2),
+                in_=words.rearrange("z p n j -> p z (n j)").bitcast(I32),
+            )
+            return codes
+
+        def xt_tile(c, i):
+            first = c * HALF + (i % 2) * P
+            return xt[i // 2][:, first : first + P].bitcast(FP8X4)
 
         load_rows(nc.sync, rows_a, XQ, xq_scales)
         load_rows(nc.scalar, rows_a, XT, xt_scales)
         load_rows(nc.sync, rows_a, WC, wc_scales)
         load_rows(nc.scalar, rows_a, WA, wa_scales)
         fr_cols = sb.tile([P, 4], F32, name="fr_cols")
-        nc.sync.dma_start(out=fr_cols[:], in_=fr.rearrange("(p j) o -> p (j o)", j=4))
+        nc.scalar.dma_start(out=fr_cols[:], in_=fr.rearrange("(p j) o -> p (j o)", j=4))
         xq = load_fp4("xq", xq_words)
         wc = load_fp8("wc", wc_words)
         wa = load_fp4("wa", wa_words)
         spread_rows([nc.sync, nc.scalar], planes_a, rows_a)
-        xt = [load_fp8("xt%d" % c, xt_words[c : c + 1]) for c in range(2)]
+        xt = [load_xt(half) for half in range(2)]
         load_rows(nc.sync, rows_b, WY, wy_scales)
         load_rows(nc.sync, rows_b, WB, wb_scales)
         wy = load_fp8("wy", wy_words)
         wb = load_fp4("wb", wb_words)
         spread_rows([nc.sync, nc.sync], planes_b, rows_b)
 
-        ident = sb.tile([P, P], F32, name="ident")
-        make_identity(nc, ident[:])
+        make_identity(nc, ident[:], nomemset=True)
 
         warm = sb.tile([P, 1], F32, name="warm")
         nc.scalar.activation(out=warm[:], in_=one[:], func=ACT.Square)
@@ -111,21 +142,30 @@ def tile_mix_hidden_by_row_energy_kernel(
         fr_ps = ps.tile([P, 4, P], F32, name="fr_ps", tag="bank7")
         for j in range(4):
             nc.tensor.transpose(fr_ps[:, j, :], fr_cols[:, j : j + 1].to_broadcast([P, P]), ident[:])
+        keep_busy(WARM_LATE)
         fr_rows = sb.tile([P, 2, P, 2], F32, name="fr_rows")
         nc.vector.tensor_copy(out=fr_rows[:], in_=fr_ps[:].rearrange("m (u e) p -> m u p e", e=2))
 
         z = [ps.tile([P, R], F32, name="z%d" % i, tag="bank%d" % i) for i in range(TILES)]
-        for i in range(TILES):
+
+        def first_small(i):
             nc.tensor.matmul_mx(
                 out=z[i][:], lhsT=fp4(xq, 0, i * P, P), lhsT_scale=plane(planes_a, XQ, i * P, P),
                 rhs=fp8(wc, 0, 0, R), rhs_scale=plane(planes_a, WC, 0, R), start=True, stop=False,
             )
-        for i in range(TILES):
+
+        def first_large(i):
             for c in range(2):
                 nc.tensor.matmul_mx(
-                    out=z[i][:], lhsT=fp8(xt[c], 0, i * P, P), lhsT_scale=plane(planes_a, XT + c, i * P, P),
+                    out=z[i][:], lhsT=xt_tile(c, i), lhsT_scale=plane(planes_a, XT + c, i * P, P),
                     rhs=fp4(wa, c, 0, R), rhs_scale=plane(planes_a, WA + c, 0, R), start=False, stop=(c == 1),
                 )
+
+        for half in range(2):
+            for i in (2 * half, 2 * half + 1):
+                first_small(i)
+            for i in (2 * half, 2 * half + 1):
+                first_large(i)
 
         squares = sb.tile([P, R], BF16, name="squares")
         total = [sb.tile([P, 1], F32, name="total%d" % i) for i in range(TILES)]
@@ -182,7 +222,7 @@ def tile_mix_hidden_by_row_energy_kernel(
                 for c in range(2):
                     nc.tensor.matmul_mx(
                         out=y[i][a // per][:, a % per, :], lhsT=fp8(wy, c, a * P, P), lhsT_scale=plane(planes_b, WY + c, a * P, P),
-                        rhs=fp8(xt[c], 0, i * P, P), rhs_scale=plane(planes_a, XT + c, i * P, P),
+                        rhs=xt_tile(c, i), rhs_scale=plane(planes_a, XT + c, i * P, P),
                         start=(a % per == 0 and c == 0), stop=False,
                     )
 
@@ -228,21 +268,21 @@ def tile_mix_hidden_by_row_energy_kernel(
         quantise(0)
         second(0)
         weigh_tile(2)
-        store(0, 0, True, nc.sync)
-        weigh_tile(3)
         quantise(1)
         turn(2)
-        turn(3)
+        store(0, 0, True, nc.sync)
         interleave(2)
-        interleave(3)
         second(1)
         skip(2)
+        weigh_tile(3)
+        turn(3)
         quantise(2)
-        store(1, 0, True, nc.sync)
-        quantise(3)
+        interleave(3)
         second(2)
-        store(2, 0, False, nc.sync)
+        store(1, 0, False, nc.sync)
         skip(3)
+        quantise(3)
+        store(2, 0, True, nc.sync)
         second(3)
-        store(3, 0, True, nc.scalar)
-        store(3, 1, False, nc.sync)
+        store(3, 0, False, nc.sync)
+        store(3, 1, True, nc.scalar)

from contextlib import ExitStack

import concourse.mybir as mybir
from concourse.masks import make_identity

K, L, T, R, N = 1024, 512, 512, 512, 512
FLOPS = 2 * T * (K * R + L * R + R * N + K * N)

F32 = mybir.dt.float32
BF16 = mybir.dt.bfloat16
I32 = mybir.dt.int32
U32 = mybir.dt.uint32
U8 = mybir.dt.uint8
FP8X4 = mybir.dt.float8_e4m3fn_x4
FP4X4 = mybir.dt.float4_e2m1fn_x4
ALU = mybir.AluOpType
ACT = mybir.ActivationFunctionType

P = 128
W = 512
TILES = T // P
HALF = T // 2
WARM_EARLY, WARM_LATE = 8, 13


def tile_mix_hidden_by_row_energy_kernel(
    tc, xt_words, xt_scales, wa_words, wa_scales, xq_words, xq_scales, wc_words, wc_scales,
    fr, wb_words, wb_scales, wy_words, wy_scales, out,
):
    nc = tc.nc

    with ExitStack() as ctx:
        sb = ctx.enter_context(tc.tile_pool(name="sb", bufs=1))
        ps = ctx.enter_context(tc.psum_pool(name="ps", bufs=1))
        ctx.enter_context(tc.manual_schedule())

        def load_rows(queue, rows, first, scales):
            passes = scales.shape[0]
            dst = rows[16:32, first * W : (first + passes) * W].bitcast(I32)
            queue.dma_start(
                out=dst.rearrange("q (z n) -> q z n", z=passes),
                in_=scales.bitcast(I32).rearrange("z q n -> q z n"),
            )

        def spread_rows(queues, planes, rows):
            for q in range(4):
                queues[q % 2].dma_start(
                    out=planes[q:P:32, :].bitcast(I32),
                    in_=rows[16 + q : 32 : 4, :].bitcast(I32),
                )

        def load_fp8(name, words):
            passes = words.shape[0]
            codes = sb.tile([P, passes * W], U32, name=name, align_bytes=64)
            nc.sync.dma_start(
                out=codes[:].bitcast(I32).rearrange("p (z n) -> p z n", z=passes),
                in_=words.rearrange("z p n j -> p z (n j)").bitcast(I32),
            )
            return codes

        def load_fp4(name, words):
            passes = words.shape[0]
            codes = sb.tile([P, passes * 2 * W], U8, name=name, align_bytes=64)
            nc.sync.dma_start(
                out=codes[:].bitcast(I32).rearrange("p (z n) -> p z n", z=passes),
                in_=words.rearrange("z p b -> p z b").bitcast(I32),
            )
            return codes

        def fp8(codes, z, first, count):
            return codes[:, z * W + first : z * W + first + count].bitcast(FP8X4)

        def fp4(codes, z, first, count):
            return codes[:, 2 * (z * W + first) : 2 * (z * W + first + count)].bitcast(FP4X4)

        def plane(planes, index, first, count):
            return planes[:, index * W + first : index * W + first + count]

        XQ, WC, XT, WA = 0, 1, 2, 4
        WY, WB = 0, 2
        rows_a = sb.tile([32, 6 * W], U8, name="rows_a")
        rows_b = sb.tile([32, 3 * W], U8, name="rows_b")
        planes_a = sb.tile([P, 6 * W], U8, name="planes_a", align_bytes=64)
        planes_b = sb.tile([P, 3 * W], U8, name="planes_b", align_bytes=64)
        idle = sb.tile([P, 4 * P], BF16, name="idle", align_bytes=64)
        idle_codes = sb.tile([P, P], U32, name="idle_codes", align_bytes=64)
        idle_scales = sb.tile([P, P], U8, name="idle_scales", align_bytes=64)
        idle_ps = ps.tile([P, P], F32, name="idle_ps", tag="bank6")
        ident = sb.tile([P, P], F32, name="ident")
        nc.vector.memset(idle[:], 1.0)
        nc.vector.memset(ident[:], 0.0)
        nc.vector.quantize_mx(out=idle_codes[:].bitcast(FP8X4), scales=idle_scales[:], in_=idle[:])

        def keep_busy(count):
            for n in range(count):
                nc.tensor.matmul_mx(
                    out=idle_ps[:], lhsT=idle_codes[:].bitcast(FP8X4), lhsT_scale=idle_scales[:],
                    rhs=idle_codes[:].bitcast(FP8X4), rhs_scale=idle_scales[:], start=True, stop=True,
                )

        keep_busy(WARM_EARLY)
        nc.vector.memset(planes_a[:].bitcast(I32), 0)
        nc.vector.memset(planes_b[:].bitcast(I32), 0)
        one = sb.tile([P, 1], F32, name="one")
        nc.vector.memset(one[:], 1.0)

        def load_xt(half):
            codes = sb.tile([P, 2 * HALF], U32, name="xt%d" % half, align_bytes=64)
            words = xt_words[:, :, half * HALF : (half + 1) * HALF, :]
            nc.sync.dma_start(
                out=codes[:].bitcast(I32).rearrange("p (z n) -> p z n", z=2),
                in_=words.rearrange("z p n j -> p z (n j)").bitcast(I32),
            )
            return codes

        def xt_tile(c, i):
            first = c * HALF + (i % 2) * P
            return xt[i // 2][:, first : first + P].bitcast(FP8X4)

        load_rows(nc.sync, rows_a, XQ, xq_scales)
        load_rows(nc.scalar, rows_a, XT, xt_scales)
        load_rows(nc.sync, rows_a, WC, wc_scales)
        load_rows(nc.scalar, rows_a, WA, wa_scales)
        fr_cols = sb.tile([P, 4], F32, name="fr_cols")
        nc.scalar.dma_start(out=fr_cols[:], in_=fr.rearrange("(p j) o -> p (j o)", j=4))
        xq = load_fp4("xq", xq_words)
        wc = load_fp8("wc", wc_words)
        wa = load_fp4("wa", wa_words)
        spread_rows([nc.sync, nc.scalar], planes_a, rows_a)
        xt = [load_xt(half) for half in range(2)]
        load_rows(nc.sync, rows_b, WY, wy_scales)
        load_rows(nc.sync, rows_b, WB, wb_scales)
        wy = load_fp8("wy", wy_words)
        wb = load_fp4("wb", wb_words)
        spread_rows([nc.sync, nc.sync], planes_b, rows_b)

        make_identity(nc, ident[:], nomemset=True)

        warm = sb.tile([P, 1], F32, name="warm")
        nc.scalar.activation(out=warm[:], in_=one[:], func=ACT.Square)

        fr_ps = ps.tile([P, 4, P], F32, name="fr_ps", tag="bank7")
        for j in range(4):
            nc.tensor.transpose(fr_ps[:, j, :], fr_cols[:, j : j + 1].to_broadcast([P, P]), ident[:])
        keep_busy(WARM_LATE)
        fr_rows = sb.tile([P, 2, P, 2], F32, name="fr_rows")
        nc.vector.tensor_copy(out=fr_rows[:], in_=fr_ps[:].rearrange("m (u e) p -> m u p e", e=2))

        z = [ps.tile([P, R], F32, name="z%d" % i, tag="bank%d" % i) for i in range(TILES)]

        def first_small(i):
            nc.tensor.matmul_mx(
                out=z[i][:], lhsT=fp4(xq, 0, i * P, P), lhsT_scale=plane(planes_a, XQ, i * P, P),
                rhs=fp8(wc, 0, 0, R), rhs_scale=plane(planes_a, WC, 0, R), start=True, stop=False,
            )

        def first_large(i):
            for c in range(2):
                nc.tensor.matmul_mx(
                    out=z[i][:], lhsT=xt_tile(c, i), lhsT_scale=plane(planes_a, XT + c, i * P, P),
                    rhs=fp4(wa, c, 0, R), rhs_scale=plane(planes_a, WA + c, 0, R), start=False, stop=(c == 1),
                )

        for half in range(2):
            for i in (2 * half, 2 * half + 1):
                first_small(i)
            for i in (2 * half, 2 * half + 1):
                first_large(i)

        squares = sb.tile([P, R], BF16, name="squares")
        total = [sb.tile([P, 1], F32, name="total%d" % i) for i in range(TILES)]
        for i in range(TILES):
            nc.scalar.activation(out=squares[:], in_=z[i][:], func=ACT.Square, accum_out=total[i][:])

        denom = [sb.tile([P, 1], F32, name="denom%d" % i) for i in range(TILES)]
        recip = [sb.tile([P, 1], F32, name="recip%d" % i) for i in range(TILES)]
        gain = [sb.tile([P, 1], F32, name="gain%d" % i) for i in range(TILES)]
        hid = [[sb.tile([P, R // 2], BF16, name="hid%d_%d" % (i, u)) for u in range(2)] for i in range(TILES)]
        grouped = [sb.tile([P, R], BF16, name="grouped%d" % i, align_bytes=64) for i in range(TILES)]
        codes = [sb.tile([P, P], U32, name="codes%d" % i, align_bytes=64) for i in range(TILES)]
        scales = [sb.tile([P, P], U8, name="scales%d" % i, align_bytes=64) for i in range(TILES)]
        Y_BANKS = [[4], [5], [6], [7, 0]]
        turned = {}
        y = {}
        out_tiles = out.rearrange("(a p) t -> p a t", p=P)

        def step_denom(i):
            nc.vector.tensor_scalar(out=denom[i][:], in0=total[i][:], scalar1=float(R), scalar2=None, op0=ALU.add)

        def step_recip(i):
            nc.vector.reciprocal(out=recip[i][:], in_=denom[i][:])

        def step_gain(i):
            nc.vector.tensor_tensor(out=gain[i][:], in0=total[i][:], in1=recip[i][:], op=ALU.mult)

        def weigh(i, u):
            nc.vector.scalar_tensor_tensor(
                out=hid[i][u][:].rearrange("t (p e) -> t p e", e=2),
                in0=z[i][:].rearrange("t (p u e) -> t u p e", u=2, e=2)[:, u],
                scalar=gain[i][:], in1=fr_rows[:, u], op0=ALU.mult, op1=ALU.mult,
            )

        def turn(i):
            turned[i] = ps.tile([P, 2, P], F32, name="turned%d" % i, tag="bank%d" % i)
            for u in range(2):
                nc.tensor.transpose(turned[i][:, u, :], hid[i][u][:].bitcast(F32), ident[:])

        def interleave(i):
            nc.scalar.copy(
                out=grouped[i][:].bitcast(F32).rearrange("p (t u) -> p t u", u=2),
                in_=turned[i][:].rearrange("p u t -> p t u"),
            )

        def quantise(i):
            nc.vector.quantize_mx(out=codes[i][:].bitcast(FP8X4), scales=scales[i][:], in_=grouped[i][:])

        def skip(i):
            banks = Y_BANKS[i]
            per = 4 // len(banks)
            y[i] = [ps.tile([P, per, P], F32, name="y%d_%d" % (i, b), tag="bank%d" % b) for b in banks]
            for a in range(4):
                for c in range(2):
                    nc.tensor.matmul_mx(
                        out=y[i][a // per][:, a % per, :], lhsT=fp8(wy, c, a * P, P), lhsT_scale=plane(planes_b, WY + c, a * P, P),
                        rhs=xt_tile(c, i), rhs_scale=plane(planes_a, XT + c, i * P, P),
                        start=(a % per == 0 and c == 0), stop=False,
                    )

        def second(i):
            per = 4 // len(y[i])
            for a in range(4):
                nc.tensor.matmul_mx(
                    out=y[i][a // per][:, a % per, :], lhsT=fp4(wb, 0, a * P, P), lhsT_scale=plane(planes_b, WB, a * P, P),
                    rhs=codes[i][:].bitcast(FP8X4), rhs_scale=scales[i][:], start=False, stop=(a % per == per - 1),
                )

        def store(i, part, on_scalar, queue):
            per = 4 // len(y[i])
            result = sb.tile([P, per, P], F32, name="result%d_%d" % (i, part))
            if on_scalar:
                nc.scalar.copy(out=result[:], in_=y[i][part][:])
            else:
                nc.vector.tensor_copy(out=result[:], in_=y[i][part][:])
            queue.dma_start(out=out_tiles[:, part * per : (part + 1) * per, i * P : (i + 1) * P], in_=result[:])

        def weigh_tile(i):
            more = i + 1 < TILES
            if more:
                step_denom(i + 1)
            weigh(i, 0)
            if more:
                step_recip(i + 1)
            weigh(i, 1)
            if more:
                step_gain(i + 1)

        step_denom(0)
        step_recip(0)
        step_gain(0)
        skip(0)
        weigh_tile(0)
        turn(0)
        interleave(0)
        skip(1)
        weigh_tile(1)
        turn(1)
        interleave(1)
        quantise(0)
        second(0)
        weigh_tile(2)
        quantise(1)
        turn(2)
        store(0, 0, True, nc.sync)
        interleave(2)
        second(1)
        skip(2)
        weigh_tile(3)
        turn(3)
        quantise(2)
        interleave(3)
        second(2)
        store(1, 0, False, nc.sync)
        skip(3)
        quantise(3)
        store(2, 0, True, nc.sync)
        second(3)
        store(3, 0, False, nc.sync)
        store(3, 1, True, nc.scalar)
